import numpy as np
import ml_dtypes


def mxq(x, axis, fmt="e4m3"):
    dtype, down = {"e4m3": (ml_dtypes.float8_e4m3fn, 7), "e5m2": (ml_dtypes.float8_e5m2, 14)}[fmt]
    v = np.moveaxis(np.asarray(x, np.float32).astype(ml_dtypes.bfloat16).astype(np.float64), axis, -1)
    blocks = v.reshape(v.shape[:-1] + (-1, 32))
    amax = np.abs(blocks).max(-1, keepdims=True)
    byte = np.maximum(np.where(amax > 0, np.frexp(amax)[1] - 1 + 127, 0) - down, 1)
    scale = np.exp2(byte - 127.0)
    codes = (blocks / scale).astype(np.float32).astype(dtype).astype(np.float64)
    return np.moveaxis((codes * scale).reshape(v.shape), -1, axis)


WIDE = False


def mx_kscale(k):
    if not WIDE:
        return np.ones(k)
    levels = np.array([10, -10, 5, -5, 0])
    if k % 512:
        return np.exp2(np.random.permutation(np.resize(levels, k // 32))).repeat(32)
    a = np.empty((k // 512, 16))
    for p in range(k // 512):
        a[p, :8] = np.random.permutation(np.resize(levels, 8))
        for g in range(8):
            far = levels[np.abs(levels - a[p, g]) >= 10]
            a[p, g + 8] = far[np.random.randint(len(far))]
    return np.exp2(a.ravel()).repeat(32)


def f64(x):
    return np.asarray(x).astype(np.float64)


def striped8(idx):
    return np.asarray(idx).reshape(8, -1, 16).transpose(0, 2, 1).reshape(128, -1).astype(np.uint16)


def unstriped8(offs):
    return offs.reshape(8, 16, -1).transpose(0, 2, 1).reshape(8, -1).astype(np.int64)


def pick8(x, idx, run):
    r = np.arange(len(x))
    return x[r[:, None], idx[r % (8 * run) // run]]


E2M1 = np.array([0.0, 0.5, 1.0, 1.5, 2.0, 3.0, 4.0, 6.0, -0.0, -0.5, -1.0, -1.5, -2.0, -3.0, -4.0, -6.0])


def pack_weight(w, fmt):
    k, n = w.shape
    w = f64(np.asarray(w, np.float32).astype(ml_dtypes.bfloat16)).reshape(k // 32, 32, n)
    amax = np.abs(w).max(1)
    if fmt == "e4m3":
        byte = np.frexp(amax)[1] - 1 + 127 - 7
    else:
        mant, ex = np.frexp(amax / 6.0)
        byte = np.where(mant > 0.5, ex, ex - 1) + 127
    byte = np.clip(np.where(amax > 0, byte, 1), 1, 254)
    scaled = (w * np.exp2(127.0 - byte)[:, None, :]).reshape(k, n).astype(np.float32)
    by_word = np.ascontiguousarray(scaled.reshape(k // 512, 128, 4, n).transpose(0, 1, 3, 2))
    if fmt == "e4m3":
        words = by_word.astype(ml_dtypes.float8_e4m3fn).view(np.uint8)
    else:
        c = by_word.astype(ml_dtypes.float4_e2m1fn).view(np.uint8) & 0xF
        words = (c[..., 0::2] | (c[..., 1::2] << 4)).reshape(k // 512, 128, 2 * n)
    return np.ascontiguousarray(words), np.ascontiguousarray(byte.astype(np.uint8).reshape(k // 512, 16, n))


def unpack_weight(words, scales, fmt):
    g, _, n = scales.shape
    words = np.ascontiguousarray(words).reshape(g, 128, n, -1)
    if fmt == "e4m3":
        vals = words.view(ml_dtypes.float8_e4m3fn).astype(np.float64)
    else:
        nib = np.empty((g, 128, n, 4), np.uint8)
        nib[..., 0::2] = words & 0xF
        nib[..., 1::2] = words >> 4
        vals = E2M1[nib]
    vals = vals * np.repeat(np.exp2(scales.astype(np.float64) - 127.0), 8, axis=1)[..., None]
    return vals.transpose(0, 1, 3, 2).reshape(g * 512, n)


D, T, U, I, J, Q, E = 512, 1024, 1024, 512, 256, 512, 256


def setup_inputs():
    n = np.random.standard_normal
    idx = np.stack([np.random.permutation(T)[:I] for _ in range(8)])
    idx2 = np.stack([np.random.permutation(I)[:J] for _ in range(8)])
    idx3 = np.stack([np.random.permutation(U)[:J] for _ in range(8)])
    idx4 = np.stack([np.random.permutation(U)[:I] for _ in range(8)])
    fd = mx_kscale(D)
    fq = mx_kscale(Q)
    keysp = pack_weight(n((D, T)) / fd[:, None], "e2m1")
    notesp = pack_weight(n((D, U)) / fd[:, None], "e4m3")
    mixp = pack_weight(n((Q, E)) * 1.0 / np.sqrt(Q) / fq[:, None], "e4m3")
    return {
        "query": (n((D, Q)) * 1.0 / np.sqrt(D) * fd[:, None]).astype(np.float32),
        "query2": (n((D, Q)) * 1.0 / np.sqrt(D) * fd[:, None]).astype(np.float32),
        "keys_words": keysp[0],
        "keys_scales": keysp[1],
        "notes_words": notesp[0],
        "notes_scales": notesp[1],
        "rowf": (np.random.uniform(0.5, 2.0, (Q, 1)) * fq[:, None]).astype(np.float32),
        "mix_words": mixp[0],
        "mix_scales": mixp[1],
        "offs": striped8(idx),
        "offs2": striped8(idx2),
        "offs3": striped8(idx3),
        "offs4": striped8(idx4),
    }


def reference(query, query2, keys_words, keys_scales, notes_words, notes_scales, rowf, mix_words, mix_scales, offs, offs2, offs3, offs4):
    idx = unstriped8(offs)
    idx2 = unstriped8(offs2)
    idx3 = unstriped8(offs3)
    idx4 = unstriped8(offs4)
    keysu = unpack_weight(keys_words, keys_scales, "e2m1")
    notesu = unpack_weight(notes_words, notes_scales, "e4m3")
    mixu = unpack_weight(mix_words, mix_scales, "e4m3")
    queryq = mxq(f64(query), 0, "e4m3")
    a = queryq.T @ keysu
    query2q = mxq(f64(query2), 0, "e4m3")
    b = query2q.T @ notesu
    ta = np.max(a, axis=1, keepdims=True)
    e1 = np.exp(pick8(a, idx, 64) - ta)
    w = pick8(e1, idx2, 64) * 4.0
    f1 = np.zeros((Q, U))
    f1[np.arange(Q)[:, None], idx3[np.arange(Q) % 512 // 64]] = w
    cc = b + f1
    g = pick8(cc, idx4, 64) - e1
    gw = g * f64(rowf)
    gwq = mxq(gw, 0, "e4m3")
    y = mixu.T @ gwq
    return y

@@ -1,0 +1,193 @@
+from contextlib import ExitStack
+
+import concourse.mybir as mybir
+
+D, T, U, I, J, Q, E = 512, 1024, 1024, 512, 256, 512, 256
+FLOPS = 2 * D * Q * T + 2 * D * Q * U + 2 * Q * E * I
+
+F32 = mybir.dt.float32
+BF16 = mybir.dt.bfloat16
+I32 = mybir.dt.int32
+U32 = mybir.dt.uint32
+U16 = mybir.dt.uint16
+U8 = mybir.dt.uint8
+FP8X4 = mybir.dt.float8_e4m3fn_x4
+FP4X4 = mybir.dt.float4_e2m1fn_x4
+ALU = mybir.AluOpType
+ACT = mybir.ActivationFunctionType
+AX = mybir.AxisListType
+
+P = 128
+PACK = 4
+BANK = 512
+HALF = I // 2
+
+
+def tile_attend_secondpickexp_twoq_mixed_kernel(tc, query, query2, keys_words, keys_scales, notes_words, notes_scales,
+                                                 rowf, mix_words, mix_scales, offs, offs2, offs3, offs4, out):
+    nc = tc.nc
+    with ExitStack() as ctx:
+        sb = ctx.enter_context(tc.tile_pool(name="sb", bufs=1))
+        ps = ctx.enter_context(tc.psum_pool(name="ps", bufs=4))
+
+        def plane(name, width, engine):
+            t = sb.tile([P, width], U8, name=name, align_bytes=64)
+            engine.memset(t[:].bitcast(I32), 0)
+            return t
+
+        def load_plane(t, src, queue):
+            for g in range(4):
+                queue.dma_start(out=t[32 * g:32 * g + 4, :].bitcast(I32), in_=src[0, 4 * g:4 * g + 4, :].bitcast(I32))
+
+        def load_list(name, src, n):
+            t = sb.tile([P, n // 16], U16, name=name)
+            nc.sync.dma_start(t[:], src)
+            return t
+
+        def load_rows(name, src):
+            halves = []
+            for c in range(2):
+                t = sb.tile([P, PACK, Q // 2], F32, name=name + str(c))
+                nc.sync.dma_start(out=t[:], in_=src.rearrange("(p j) q -> p j q", j=PACK)[:, :, c * (Q // 2):(c + 1) * (Q // 2)])
+                halves.append(t)
+            return halves
+
+        def dealt_views(grouped, halves, c):
+            dst = grouped[:].rearrange("p (r m j) -> p m r j", r=PACK, j=PACK)[:, c * (P // 2):(c + 1) * (P // 2)]
+            return dst, halves[c][:].rearrange("p j (m r) -> p m r j", r=PACK)
+
+        k_plane = plane("k_plane", T, nc.vector)
+        load_plane(k_plane, keys_scales, nc.scalar)
+        q_raw = load_rows("q_raw", query)
+        k_words = sb.tile([P, 2 * T], U8, name="k_words", align_bytes=64)
+        nc.sync.dma_start(out=k_words[:].bitcast(I32), in_=keys_words[0].bitcast(I32))
+        idx = load_list("idx", offs, I)
+        n_plane = plane("n_plane", U, nc.vector)
+        m_plane = plane("m_plane", E, nc.vector)
+        q2_raw = load_rows("q2_raw", query2)
+        idx2 = load_list("idx2", offs2, J)
+        n_words = sb.tile([P, U], I32, name="n_words", align_bytes=64)
+        nc.sync.dma_start(out=n_words[:], in_=notes_words[0].rearrange("p n t -> p (n t)").bitcast(I32))
+        load_plane(n_plane, notes_scales, nc.sync)
+        idx3 = load_list("idx3", offs3, J)
+        idx4 = load_list("idx4", offs4, I)
+        rf = sb.tile([P, PACK], F32, name="rf")
+        nc.sync.dma_start(out=rf[:], in_=rowf.rearrange("(p r) o -> p (r o)", r=PACK))
+        m_words = sb.tile([P, E], I32, name="m_words", align_bytes=64)
+        nc.sync.dma_start(out=m_words[:], in_=mix_words[0].rearrange("p n t -> p (n t)").bitcast(I32))
+        load_plane(m_plane, mix_scales, nc.sync)
+
+        f1 = []
+        for s in range(2):
+            t = sb.tile([P, U], F32, name="f1_" + str(s))
+            nc.vector.memset(t[:], 0.0)
+            f1.append(t)
+
+        q_bf = sb.tile([P, PACK * Q], BF16, name="q_bf", align_bytes=64)
+        q_codes = sb.tile([P, Q], U32, name="q_codes", align_bytes=64)
+        q_plane = sb.tile([P, Q], U8, name="q_plane", align_bytes=64)
+        dst, src = dealt_views(q_bf, q_raw, 0)
+        nc.vector.tensor_copy(out=dst, in_=src)
+        dst, src = dealt_views(q_bf, q_raw, 1)
+        nc.vector.tensor_copy(out=dst[:, :44], in_=src[:, :44])
+        nc.scalar.copy(out=dst[:, 44:], in_=src[:, 44:])
+        nc.vector.quantize_mx(out=q_codes[:, :P].bitcast(FP8X4), scales=q_plane[:, :P], in_=q_bf[:, :PACK * P])
+        nc.vector.quantize_mx(out=q_codes[:, P:].bitcast(FP8X4), scales=q_plane[:, P:], in_=q_bf[:, PACK * P:])
+
+        q2_bf = sb.tile([P, PACK * Q], BF16, name="q2_bf", align_bytes=64)
+        q2_codes = sb.tile([P, Q], U32, name="q2_codes", align_bytes=64)
+        q2_plane = sb.tile([P, Q], U8, name="q2_plane", align_bytes=64)
+
+        a = [sb.tile([P, T], F32, name="a" + str(r)) for r in range(PACK)]
+        tops = [sb.tile([P, 2], F32, name="tops" + str(r)) for r in range(PACK)]
+        neg_ta = [sb.tile([P, 1], F32, name="neg_ta" + str(r)) for r in range(PACK)]
+        e1 = [sb.tile([P, I], F32, name="e1_" + str(r)) for r in range(PACK)]
+        w = [sb.tile([P, J], F32, name="w" + str(r)) for r in range(PACK)]
+        cc = [sb.tile([P, U], F32, name="cc" + str(r)) for r in range(PACK)]
+        picked = [sb.tile([P, I], F32, name="picked" + str(r)) for r in range(PACK - 1)]
+        g = [sb.tile([P, I], F32, name="g" + str(r)) for r in range(PACK)]
+        gw3 = sb.tile([P, PACK - 1, I], BF16, name="gw3")
+        gw = sb.tile([P, I, PACK], BF16, name="gw", align_bytes=64)
+        gw_codes = sb.tile([P, I], U32, name="gw_codes", align_bytes=64)
+        gw_plane = sb.tile([P, I], U8, name="gw_plane", align_bytes=64)
+
+        def token_scores(r):
+            rows = slice(r * P, (r + 1) * P)
+            for h in range(2):
+                bank = ps.tile([P, BANK], F32, name="a_bank")
+                nc.tensor.matmul_mx(out=bank[:], lhsT=q_codes[:, rows].bitcast(FP8X4), lhsT_scale=q_plane[:, rows],
+                                    rhs=k_words[:, 2 * h * BANK:2 * (h + 1) * BANK].bitcast(FP4X4),
+                                    rhs_scale=k_plane[:, h * BANK:(h + 1) * BANK], start=True, stop=True)
+                nc.vector.tensor_scalar(out=a[r][:, h * BANK:(h + 1) * BANK], in0=bank[:], scalar1=1.0, scalar2=None,
+                                        op0=ALU.mult, op1=ALU.max, accum_out=tops[r][:, h:h + 1])
+            nc.vector.tensor_reduce(out=neg_ta[r][:], in_=tops[r][:], axis=AX.X, op=ALU.max, negate=True)
+
+        def picks(r):
+            nc.scalar.activation(out=e1[r][:], in_=a[r][:].indirect(idx[:]), func=ACT.Exp, bias=neg_ta[r][:])
+            nc.scalar.activation(out=w[r][:], in_=e1[r][:].indirect(idx2[:]), func=ACT.Copy, scale=4.0)
+
+        def scatter(r):
+            nc.vector.tensor_copy(out=f1[r % 2][:].indirect(idx3[:]), in_=w[r][:])
+
+        def note_scores(r):
+            rows = slice(r * P, (r + 1) * P)
+            for h in range(2):
+                cols = slice(h * BANK, (h + 1) * BANK)
+                bank = ps.tile([P, BANK], F32, name="b_bank")
+                nc.tensor.matmul_mx(out=bank[:], lhsT=q2_codes[:, rows].bitcast(FP8X4), lhsT_scale=q2_plane[:, rows],
+                                    rhs=n_words[:, cols].bitcast(FP8X4), rhs_scale=n_plane[:, cols], start=True, stop=True)
+                nc.vector.tensor_tensor(out=cc[r][:, cols], in0=bank[:], in1=f1[r % 2][:, cols], op=ALU.add)
+
+        def result(r):
+            nc.scalar.activation(out=picked[r][:], in_=cc[r][:].indirect(idx4[:]), func=ACT.Copy)
+            nc.gpsimd.tensor_tensor(out=g[r][:], in0=picked[r][:], in1=e1[r][:], op=ALU.subtract)
+            nc.scalar.activation(out=gw3[:, r, :], in_=g[r][:], func=ACT.Copy, scale=rf[:, r:r + 1])
+
+        token_scores(0)
+        picks(0)
+        token_scores(1)
+        picks(1)
+        for c in range(2):
+            dst, src = dealt_views(q2_bf, q2_raw, c)
+            nc.gpsimd.tensor_scalar(out=dst, in0=src, scalar1=1.0, scalar2=0.0, op0=ALU.mult, op1=ALU.add)
+        token_scores(2)
+        picks(2)
+        scatter(0)
+        nc.vector.quantize_mx(out=q2_codes[:].bitcast(FP8X4), scales=q2_plane[:], in_=q2_bf[:])
+        token_scores(3)
+        picks(3)
+        scatter(1)
+        note_scores(0)
+        result(0)
+        note_scores(1)
+        result(1)
+        scatter(2)
+        note_scores(2)
+        result(2)
+        scatter(3)
+        note_scores(3)
+        nc.vector.tensor_copy(out=gw[:, :, :PACK - 1], in_=gw3[:].rearrange("p r i -> p i r"))
+
+        last = PACK - 1
+        lo, hi = slice(0, HALF), slice(HALF, I)
+        picked_hi = sb.tile([P, HALF], F32, name="picked_hi")
+        nc.vector.tensor_tensor(out=g[last][:, lo], in0=cc[last][:].indirect(idx4[:, :HALF // 16]), in1=e1[last][:, lo], op=ALU.subtract)
+        nc.scalar.activation(out=picked_hi[:], in_=cc[last][:].indirect(idx4[:, HALF // 16:]), func=ACT.Copy)
+        nc.vector.tensor_tensor(out=g[last][:, hi], in0=picked_hi[:], in1=e1[last][:, hi], op=ALU.subtract)
+        for slots in (lo, hi):
+            nc.vector.tensor_scalar(out=gw[:, slots, last], in0=g[last][:, slots], scalar1=rf[:, last:], scalar2=None, op0=ALU.mult)
+        for h, slots in enumerate((lo, hi)):
+            nc.vector.quantize_mx(out=gw_codes[:, slots].bitcast(FP8X4), scales=gw_plane[:, slots],
+                                  in_=gw[:, slots, :].rearrange("p i r -> p (i r)"))
+        for h, slots in enumerate((lo, hi)):
+            for t in range(2):
+                cols = slice(t * P, (t + 1) * P)
+                bank = ps.tile([P, HALF], F32, name="a_bank")
+                nc.tensor.matmul_mx(out=bank[:], lhsT=m_words[:, cols].bitcast(FP8X4), lhsT_scale=m_plane[:, cols],
+                                    rhs=gw_codes[:, slots].bitcast(FP8X4), rhs_scale=gw_plane[:, slots], start=True, stop=True)
+                y = sb.tile([P, HALF], F32, name="y" + str(2 * h + t))
+                if h == 1 and t == 1:
+                    nc.vector.tensor_copy(out=y[:], in_=bank[:])
+                else:
+                    nc.scalar.copy(out=y[:], in_=bank[:])
+                nc.sync.dma_start(out=out[cols, slots], in_=y[:])

@@ -106,7 +106,7 @@ def tile_attend_secondpickexp_twoq_mixed_kernel(tc, query, query2, keys_words, k
         cc = [sb.tile([P, U], F32, name="cc" + str(r)) for r in range(PACK)]
         picked = [sb.tile([P, I], F32, name="picked" + str(r)) for r in range(PACK - 1)]
         g = [sb.tile([P, I], F32, name="g" + str(r)) for r in range(PACK)]
-        gw3 = sb.tile([P, PACK - 1, I], BF16, name="gw3")
+        gw4 = sb.tile([P, PACK, I], BF16, name="gw4")
         gw = sb.tile([P, I, PACK], BF16, name="gw", align_bytes=64)
         gw_codes = sb.tile([P, I], U32, name="gw_codes", align_bytes=64)
         gw_plane = sb.tile([P, I], U8, name="gw_plane", align_bytes=64)
@@ -126,8 +126,10 @@ def tile_attend_secondpickexp_twoq_mixed_kernel(tc, query, query2, keys_words, k
             nc.scalar.activation(out=e1[r][:], in_=a[r][:].indirect(idx[:]), func=ACT.Exp, bias=neg_ta[r][:])
             nc.scalar.activation(out=w[r][:], in_=e1[r][:].indirect(idx2[:]), func=ACT.Copy, scale=4.0)
 
+        window = (0, 1, 0, 0)
+
         def scatter(r):
-            nc.vector.tensor_copy(out=f1[r % 2][:].indirect(idx3[:]), in_=w[r][:])
+            nc.vector.tensor_copy(out=f1[window[r]][:].indirect(idx3[:]), in_=w[r][:])
 
         def note_scores(r):
             rows = slice(r * P, (r + 1) * P)
@@ -136,49 +138,52 @@ def tile_attend_secondpickexp_twoq_mixed_kernel(tc, query, query2, keys_words, k
                 bank = ps.tile([P, BANK], F32, name="b_bank")
                 nc.tensor.matmul_mx(out=bank[:], lhsT=q2_codes[:, rows].bitcast(FP8X4), lhsT_scale=q2_plane[:, rows],
                                     rhs=n_words[:, cols].bitcast(FP8X4), rhs_scale=n_plane[:, cols], start=True, stop=True)
-                nc.vector.tensor_tensor(out=cc[r][:, cols], in0=bank[:], in1=f1[r % 2][:, cols], op=ALU.add)
+                nc.vector.tensor_tensor(out=cc[r][:, cols], in0=bank[:], in1=f1[window[r]][:, cols], op=ALU.add)
 
         def result(r):
             nc.scalar.activation(out=picked[r][:], in_=cc[r][:].indirect(idx4[:]), func=ACT.Copy)
             nc.gpsimd.tensor_tensor(out=g[r][:], in0=picked[r][:], in1=e1[r][:], op=ALU.subtract)
-            nc.scalar.activation(out=gw3[:, r, :], in_=g[r][:], func=ACT.Copy, scale=rf[:, r:r + 1])
+            nc.gpsimd.tensor_scalar(out=gw4[:, r, :], in0=g[r][:], scalar1=rf[:, r:r + 1], scalar2=0.0, op0=ALU.mult, op1=ALU.add)
 
-        token_scores(0)
-        picks(0)
-        token_scores(1)
-        picks(1)
         for c in range(2):
             dst, src = dealt_views(q2_bf, q2_raw, c)
             nc.gpsimd.tensor_scalar(out=dst, in0=src, scalar1=1.0, scalar2=0.0, op0=ALU.mult, op1=ALU.add)
-        token_scores(2)
-        picks(2)
-        scatter(0)
+        for r in range(PACK):
+            token_scores(r)
+            picks(r)
         nc.vector.quantize_mx(out=q2_codes[:].bitcast(FP8X4), scales=q2_plane[:], in_=q2_bf[:])
-        token_scores(3)
-        picks(3)
+        scatter(0)
         scatter(1)
-        note_scores(0)
-        result(0)
-        note_scores(1)
-        result(1)
-        scatter(2)
-        note_scores(2)
-        result(2)
-        scatter(3)
-        note_scores(3)
-        nc.vector.tensor_copy(out=gw[:, :, :PACK - 1], in_=gw3[:].rearrange("p r i -> p i r"))
+        for r in range(PACK):
+            if r > 1:
+                scatter(r)
+            note_scores(r)
+            if r < PACK - 1:
+                result(r)
 
         last = PACK - 1
         lo, hi = slice(0, HALF), slice(HALF, I)
         picked_hi = sb.tile([P, HALF], F32, name="picked_hi")
         nc.vector.tensor_tensor(out=g[last][:, lo], in0=cc[last][:].indirect(idx4[:, :HALF // 16]), in1=e1[last][:, lo], op=ALU.subtract)
         nc.scalar.activation(out=picked_hi[:], in_=cc[last][:].indirect(idx4[:, HALF // 16:]), func=ACT.Copy)
-        nc.vector.tensor_tensor(out=g[last][:, hi], in0=picked_hi[:], in1=e1[last][:, hi], op=ALU.subtract)
-        for slots in (lo, hi):
-            nc.vector.tensor_scalar(out=gw[:, slots, last], in0=g[last][:, slots], scalar1=rf[:, last:], scalar2=None, op0=ALU.mult)
-        for h, slots in enumerate((lo, hi)):
+
+        def weigh_last(slots):
+            nc.vector.tensor_scalar(out=gw4[:, last, slots], in0=g[last][:, slots], scalar1=rf[:, last:], scalar2=None, op0=ALU.mult)
+
+        def weave(slots):
+            nc.vector.tensor_copy(out=gw[:, slots, :], in_=gw4[:, :, slots].rearrange("p r i -> p i r"))
+
+        def quantise(slots):
             nc.vector.quantize_mx(out=gw_codes[:, slots].bitcast(FP8X4), scales=gw_plane[:, slots],
                                   in_=gw[:, slots, :].rearrange("p i r -> p (i r)"))
+
+        nc.vector.tensor_tensor(out=g[last][:, hi], in0=picked_hi[:], in1=e1[last][:, hi], op=ALU.subtract)
+        weigh_last(lo)
+        weigh_last(hi)
+        weave(lo)
+        weave(hi)
+        quantise(lo)
+        quantise(hi)
         for h, slots in enumerate((lo, hi)):
             for t in range(2):
                 cols = slice(t * P, (t + 1) * P)

from contextlib import ExitStack

import concourse.mybir as mybir

D, T, U, I, J, Q, E = 512, 1024, 1024, 512, 256, 512, 256
FLOPS = 2 * D * Q * T + 2 * D * Q * U + 2 * Q * E * I

F32 = mybir.dt.float32
BF16 = mybir.dt.bfloat16
I32 = mybir.dt.int32
U32 = mybir.dt.uint32
U16 = mybir.dt.uint16
U8 = mybir.dt.uint8
FP8X4 = mybir.dt.float8_e4m3fn_x4
FP4X4 = mybir.dt.float4_e2m1fn_x4
ALU = mybir.AluOpType
ACT = mybir.ActivationFunctionType
AX = mybir.AxisListType

P = 128
PACK = 4
BANK = 512
HALF = I // 2


def tile_attend_secondpickexp_twoq_mixed_kernel(tc, query, query2, keys_words, keys_scales, notes_words, notes_scales,
                                                 rowf, mix_words, mix_scales, offs, offs2, offs3, offs4, out):
    nc = tc.nc
    with ExitStack() as ctx:
        sb = ctx.enter_context(tc.tile_pool(name="sb", bufs=1))
        ps = ctx.enter_context(tc.psum_pool(name="ps", bufs=4))

        def plane(name, width, engine):
            t = sb.tile([P, width], U8, name=name, align_bytes=64)
            engine.memset(t[:].bitcast(I32), 0)
            return t

        def load_plane(t, src, queue):
            for g in range(4):
                queue.dma_start(out=t[32 * g:32 * g + 4, :].bitcast(I32), in_=src[0, 4 * g:4 * g + 4, :].bitcast(I32))

        def load_list(name, src, n):
            t = sb.tile([P, n // 16], U16, name=name)
            nc.sync.dma_start(t[:], src)
            return t

        def load_rows(name, src):
            halves = []
            for c in range(2):
                t = sb.tile([P, PACK, Q // 2], F32, name=name + str(c))
                nc.sync.dma_start(out=t[:], in_=src.rearrange("(p j) q -> p j q", j=PACK)[:, :, c * (Q // 2):(c + 1) * (Q // 2)])
                halves.append(t)
            return halves

        def dealt_views(grouped, halves, c):
            dst = grouped[:].rearrange("p (r m j) -> p m r j", r=PACK, j=PACK)[:, c * (P // 2):(c + 1) * (P // 2)]
            return dst, halves[c][:].rearrange("p j (m r) -> p m r j", r=PACK)

        k_plane = plane("k_plane", T, nc.vector)
        load_plane(k_plane, keys_scales, nc.scalar)
        q_raw = load_rows("q_raw", query)
        k_words = sb.tile([P, 2 * T], U8, name="k_words", align_bytes=64)
        nc.sync.dma_start(out=k_words[:].bitcast(I32), in_=keys_words[0].bitcast(I32))
        idx = load_list("idx", offs, I)
        n_plane = plane("n_plane", U, nc.vector)
        m_plane = plane("m_plane", E, nc.vector)
        q2_raw = load_rows("q2_raw", query2)
        idx2 = load_list("idx2", offs2, J)
        n_words = sb.tile([P, U], I32, name="n_words", align_bytes=64)
        nc.sync.dma_start(out=n_words[:], in_=notes_words[0].rearrange("p n t -> p (n t)").bitcast(I32))
        load_plane(n_plane, notes_scales, nc.sync)
        idx3 = load_list("idx3", offs3, J)
        idx4 = load_list("idx4", offs4, I)
        rf = sb.tile([P, PACK], F32, name="rf")
        nc.sync.dma_start(out=rf[:], in_=rowf.rearrange("(p r) o -> p (r o)", r=PACK))
        m_words = sb.tile([P, E], I32, name="m_words", align_bytes=64)
        nc.sync.dma_start(out=m_words[:], in_=mix_words[0].rearrange("p n t -> p (n t)").bitcast(I32))
        load_plane(m_plane, mix_scales, nc.sync)

        f1 = []
        for s in range(2):
            t = sb.tile([P, U], F32, name="f1_" + str(s))
            nc.vector.memset(t[:], 0.0)
            f1.append(t)

        q_bf = sb.tile([P, PACK * Q], BF16, name="q_bf", align_bytes=64)
        q_codes = sb.tile([P, Q], U32, name="q_codes", align_bytes=64)
        q_plane = sb.tile([P, Q], U8, name="q_plane", align_bytes=64)
        dst, src = dealt_views(q_bf, q_raw, 0)
        nc.vector.tensor_copy(out=dst, in_=src)
        dst, src = dealt_views(q_bf, q_raw, 1)
        nc.vector.tensor_copy(out=dst[:, :44], in_=src[:, :44])
        nc.scalar.copy(out=dst[:, 44:], in_=src[:, 44:])
        nc.vector.quantize_mx(out=q_codes[:, :P].bitcast(FP8X4), scales=q_plane[:, :P], in_=q_bf[:, :PACK * P])
        nc.vector.quantize_mx(out=q_codes[:, P:].bitcast(FP8X4), scales=q_plane[:, P:], in_=q_bf[:, PACK * P:])

        q2_bf = sb.tile([P, PACK * Q], BF16, name="q2_bf", align_bytes=64)
        q2_codes = sb.tile([P, Q], U32, name="q2_codes", align_bytes=64)
        q2_plane = sb.tile([P, Q], U8, name="q2_plane", align_bytes=64)

        a = [sb.tile([P, T], F32, name="a" + str(r)) for r in range(PACK)]
        tops = [sb.tile([P, 2], F32, name="tops" + str(r)) for r in range(PACK)]
        neg_ta = [sb.tile([P, 1], F32, name="neg_ta" + str(r)) for r in range(PACK)]
        e1 = [sb.tile([P, I], F32, name="e1_" + str(r)) for r in range(PACK)]
        w = [sb.tile([P, J], F32, name="w" + str(r)) for r in range(PACK)]
        cc = [sb.tile([P, U], F32, name="cc" + str(r)) for r in range(PACK)]
        picked = [sb.tile([P, I], F32, name="picked" + str(r)) for r in range(PACK - 1)]
        g = [sb.tile([P, I], F32, name="g" + str(r)) for r in range(PACK)]
        gw4 = sb.tile([P, PACK, I], BF16, name="gw4")
        gw = sb.tile([P, I, PACK], BF16, name="gw", align_bytes=64)
        gw_codes = sb.tile([P, I], U32, name="gw_codes", align_bytes=64)
        gw_plane = sb.tile([P, I], U8, name="gw_plane", align_bytes=64)

        def token_scores(r):
            rows = slice(r * P, (r + 1) * P)
            for h in range(2):
                bank = ps.tile([P, BANK], F32, name="a_bank")
                nc.tensor.matmul_mx(out=bank[:], lhsT=q_codes[:, rows].bitcast(FP8X4), lhsT_scale=q_plane[:, rows],
                                    rhs=k_words[:, 2 * h * BANK:2 * (h + 1) * BANK].bitcast(FP4X4),
                                    rhs_scale=k_plane[:, h * BANK:(h + 1) * BANK], start=True, stop=True)
                nc.vector.tensor_scalar(out=a[r][:, h * BANK:(h + 1) * BANK], in0=bank[:], scalar1=1.0, scalar2=None,
                                        op0=ALU.mult, op1=ALU.max, accum_out=tops[r][:, h:h + 1])
            nc.vector.tensor_reduce(out=neg_ta[r][:], in_=tops[r][:], axis=AX.X, op=ALU.max, negate=True)

        def picks(r):
            nc.scalar.activation(out=e1[r][:], in_=a[r][:].indirect(idx[:]), func=ACT.Exp, bias=neg_ta[r][:])
            nc.scalar.activation(out=w[r][:], in_=e1[r][:].indirect(idx2[:]), func=ACT.Copy, scale=4.0)

        window = (0, 1, 0, 0)

        def scatter(r):
            nc.vector.tensor_copy(out=f1[window[r]][:].indirect(idx3[:]), in_=w[r][:])

        def note_scores(r):
            rows = slice(r * P, (r + 1) * P)
            for h in range(2):
                cols = slice(h * BANK, (h + 1) * BANK)
                bank = ps.tile([P, BANK], F32, name="b_bank")
                nc.tensor.matmul_mx(out=bank[:], lhsT=q2_codes[:, rows].bitcast(FP8X4), lhsT_scale=q2_plane[:, rows],
                                    rhs=n_words[:, cols].bitcast(FP8X4), rhs_scale=n_plane[:, cols], start=True, stop=True)
                nc.vector.tensor_tensor(out=cc[r][:, cols], in0=bank[:], in1=f1[window[r]][:, cols], op=ALU.add)

        def result(r):
            nc.scalar.activation(out=picked[r][:], in_=cc[r][:].indirect(idx4[:]), func=ACT.Copy)
            nc.gpsimd.tensor_tensor(out=g[r][:], in0=picked[r][:], in1=e1[r][:], op=ALU.subtract)
            nc.gpsimd.tensor_scalar(out=gw4[:, r, :], in0=g[r][:], scalar1=rf[:, r:r + 1], scalar2=0.0, op0=ALU.mult, op1=ALU.add)

        for c in range(2):
            dst, src = dealt_views(q2_bf, q2_raw, c)
            nc.gpsimd.tensor_scalar(out=dst, in0=src, scalar1=1.0, scalar2=0.0, op0=ALU.mult, op1=ALU.add)
        for r in range(PACK):
            token_scores(r)
            picks(r)
        nc.vector.quantize_mx(out=q2_codes[:].bitcast(FP8X4), scales=q2_plane[:], in_=q2_bf[:])
        scatter(0)
        scatter(1)
        for r in range(PACK):
            if r > 1:
                scatter(r)
            note_scores(r)
            if r < PACK - 1:
                result(r)

        last = PACK - 1
        lo, hi = slice(0, HALF), slice(HALF, I)
        picked_hi = sb.tile([P, HALF], F32, name="picked_hi")
        nc.vector.tensor_tensor(out=g[last][:, lo], in0=cc[last][:].indirect(idx4[:, :HALF // 16]), in1=e1[last][:, lo], op=ALU.subtract)
        nc.scalar.activation(out=picked_hi[:], in_=cc[last][:].indirect(idx4[:, HALF // 16:]), func=ACT.Copy)

        def weigh_last(slots):
            nc.vector.tensor_scalar(out=gw4[:, last, slots], in0=g[last][:, slots], scalar1=rf[:, last:], scalar2=None, op0=ALU.mult)

        def weave(slots):
            nc.vector.tensor_copy(out=gw[:, slots, :], in_=gw4[:, :, slots].rearrange("p r i -> p i r"))

        def quantise(slots):
            nc.vector.quantize_mx(out=gw_codes[:, slots].bitcast(FP8X4), scales=gw_plane[:, slots],
                                  in_=gw[:, slots, :].rearrange("p i r -> p (i r)"))

        nc.vector.tensor_tensor(out=g[last][:, hi], in0=picked_hi[:], in1=e1[last][:, hi], op=ALU.subtract)
        weigh_last(lo)
        weigh_last(hi)
        weave(lo)
        weave(hi)
        quantise(lo)
        quantise(hi)
        for h, slots in enumerate((lo, hi)):
            for t in range(2):
                cols = slice(t * P, (t + 1) * P)
                bank = ps.tile([P, HALF], F32, name="a_bank")
                nc.tensor.matmul_mx(out=bank[:], lhsT=m_words[:, cols].bitcast(FP8X4), lhsT_scale=m_plane[:, cols],
                                    rhs=gw_codes[:, slots].bitcast(FP8X4), rhs_scale=gw_plane[:, slots], start=True, stop=True)
                y = sb.tile([P, HALF], F32, name="y" + str(2 * h + t))
                if h == 1 and t == 1:
                    nc.vector.tensor_copy(out=y[:], in_=bank[:])
                else:
                    nc.scalar.copy(out=y[:], in_=bank[:])
                nc.sync.dma_start(out=out[cols, slots], in_=y[:])
